import numpy as np
import ml_dtypes


def mxq(x, axis, fmt="e4m3"):
    dtype, down = {"e4m3": (ml_dtypes.float8_e4m3fn, 7), "e5m2": (ml_dtypes.float8_e5m2, 14)}[fmt]
    v = np.moveaxis(np.asarray(x, np.float32).astype(ml_dtypes.bfloat16).astype(np.float64), axis, -1)
    blocks = v.reshape(v.shape[:-1] + (-1, 32))
    amax = np.abs(blocks).max(-1, keepdims=True)
    byte = np.maximum(np.where(amax > 0, np.frexp(amax)[1] - 1 + 127, 0) - down, 1)
    scale = np.exp2(byte - 127.0)
    codes = (blocks / scale).astype(np.float32).astype(dtype).astype(np.float64)
    return np.moveaxis((codes * scale).reshape(v.shape), -1, axis)


WIDE = False


def mx_kscale(k):
    if not WIDE:
        return np.ones(k)
    levels = np.array([10, -10, 5, -5, 0])
    if k % 512:
        return np.exp2(np.random.permutation(np.resize(levels, k // 32))).repeat(32)
    a = np.empty((k // 512, 16))
    for p in range(k // 512):
        a[p, :8] = np.random.permutation(np.resize(levels, 8))
        for g in range(8):
            far = levels[np.abs(levels - a[p, g]) >= 10]
            a[p, g + 8] = far[np.random.randint(len(far))]
    return np.exp2(a.ravel()).repeat(32)


def f64(x):
    return np.asarray(x).astype(np.float64)


def striped(idx):
    return np.tile(idx.reshape(-1, 16).T, (8, 1)).astype(np.uint16)


def unstriped(offs):
    return offs[:16].T.reshape(-1).astype(np.int64)


def silu(v):
    return v / (1.0 + np.exp(-np.maximum(v, -700.0)))


K, T, D, S, V, H, N = 1536, 1024, 2, 512, 256, 1024, 256


def setup_inputs():
    n = np.random.standard_normal
    s = mx_kscale(K)[:, None]
    u = mx_kscale(H)
    return {
        "xT": (n((K, T)) * s).astype(np.float32),
        "w1": (n((K, H)) / np.sqrt(K) / s * u).astype(np.float32),
        "w2": (n((H, N)) / np.sqrt(H) / u[:, None]).astype(np.float32),
        "gate": np.tile(np.random.uniform(0.5, 1.5, V), (N, 1)).astype(np.float32),
        "offs": striped(np.random.permutation(T)[:S]),
        "pos1": striped(np.random.permutation(2 * V)[:V]),
    }


def reference(xT, w1, w2, gate, offs, pos1):
    h = silu(mxq(f64(w1), 0, "e4m3").T @ mxq(f64(xT)[:, unstriped(offs)], 0, "e4m3"))
    z = h.reshape(H, V, D).max(axis=2)
    out = np.zeros((N, 2 * V))
    out[:, unstriped(pos1)] = f64(gate) * (mxq(f64(w2), 0, "e4m3").T @ mxq(z, 0, "e4m3"))
    return out

@@ -1,0 +1,186 @@
+from contextlib import ExitStack
+
+import concourse.mybir as mybir
+
+K, T, D, S, V, H, N = 1536, 1024, 2, 512, 256, 1024, 256
+FLOPS = 2 * K * S * H + 2 * H * V * N
+
+F32 = mybir.dt.float32
+BF16 = mybir.dt.bfloat16
+U32 = mybir.dt.uint32
+U16 = mybir.dt.uint16
+U8 = mybir.dt.uint8
+FP8X4 = mybir.dt.float8_e4m3fn_x4
+SILU = mybir.ActivationFunctionType.Silu
+COPY = mybir.ActivationFunctionType.Copy
+MULT = mybir.AluOpType.mult
+MAX = mybir.AluOpType.max
+
+P = 128
+PASSES = K // 512
+GROUPS = H // 512
+X_LOADS = ((0, 256), (256, 256), (512, 512))
+X_LOADS_LATER = ((0, 512), (512, 512))
+X_SCALAR = 5 / 8
+W_SCALAR = 80
+W_SCALAR_LAST = 56
+
+
+def tile_picked_vpool_silu_e_kernel(tc, xT, w1, w2, gate, offs, pos1, out):
+    nc = tc.nc
+    with ExitStack() as ctx:
+        keep = ctx.enter_context(tc.tile_pool(name="keep", bufs=1))
+        psum = ctx.enter_context(tc.psum_pool(name="psum", bufs=1))
+
+        offs_t = keep.tile([P, S // 16], U16, name="offs_t")
+        pos_t = keep.tile([P, V // 16], U16, name="pos_t")
+        x_loads = [X_LOADS if s == 0 else X_LOADS_LATER for s in range(PASSES)]
+        x_raw = [[keep.tile([P, 4, n], F32, name=f"x_raw{s}_{t0}") for t0, n in x_loads[s]] for s in range(PASSES)]
+        w_raw = [[keep.tile([P, 4, 512], F32, name=f"w_raw{g}_{s}") for s in range(PASSES)] for g in range(GROUPS)]
+        w2_raw = keep.tile([P, GROUPS, 4, N], F32, name="w2_raw")
+        gate_t = keep.tile([P, N // P, V], F32, name="gate_t")
+
+        warm = keep.tile([P, 1], F32, name="warm")
+        warm_out = keep.tile([P, 1], F32, name="warm_out")
+        nc.gpsimd.memset(warm[:], 0.0)
+        nc.scalar.activation(warm_out[:], warm[:], SILU)
+
+        x_scales = keep.tile([P, T], U8, name="x_scales", align_bytes=64)
+        nc.gpsimd.memset(x_scales[:], 0)
+        placed = [keep.tile([P, 2 * V], F32, name=f"placed{a}") for a in range(N // P)]
+        for a in range(N // P):
+            nc.gpsimd.memset(placed[a][:], 0.0)
+
+        for s in range(PASSES):
+            for a, (t0, n) in enumerate(x_loads[s]):
+                nc.sync.dma_start(
+                    out=x_raw[s][a][:],
+                    in_=xT[512 * s : 512 * (s + 1), t0 : t0 + n].rearrange("(p j) t -> p j t", j=4),
+                )
+                if s == 0 and a == 1:
+                    nc.sync.dma_start(offs_t[:], offs)
+        for g in range(GROUPS):
+            for s in range(PASSES):
+                nc.sync.dma_start(
+                    out=w_raw[g][s][:],
+                    in_=w1[512 * s : 512 * (s + 1), 512 * g : 512 * (g + 1)].rearrange("(p j) c -> p j c", j=4),
+                )
+        nc.sync.dma_start(out=w2_raw[:], in_=w2.rearrange("(g p j) n -> p g j n", g=GROUPS, j=4))
+        nc.sync.dma_start(pos_t[:], pos1)
+        nc.sync.dma_start(out=gate_t[:], in_=gate.rearrange("(a p) v -> p a v", p=P))
+
+        xg_codes = []
+        for s in range(PASSES):
+            x_codes = keep.tile([P, T], U32, name=f"x_codes{s}", align_bytes=64)
+            for a, (t0, n) in enumerate(x_loads[s]):
+                xb = keep.tile([P, n, 4], BF16, name=f"xb{s}_{a}", align_bytes=64)
+                dst = xb[:].rearrange("p (c i) j -> p c j i", i=4)
+                src = x_raw[s][a][:].rearrange("p j (c i) -> p c j i", i=4)
+                cut = int(n * X_SCALAR) // 4
+                nc.scalar.activation(dst[:, 0:cut], src[:, 0:cut], COPY)
+                nc.vector.tensor_copy(dst[:, cut : n // 4], src[:, cut : n // 4])
+                cols = slice(t0, t0 + n)
+                nc.vector.quantize_mx(
+                    out=x_codes[:, cols].bitcast(FP8X4),
+                    scales=x_scales[4 * s : P, cols],
+                    in_=xb[:].rearrange("p t j -> p (t j)"),
+                )
+            picked = keep.tile([P, S], U32, name=f"xg_codes{s}", align_bytes=64)
+            nc.vector.tensor_copy(picked[:], x_codes[:].indirect(offs_t[:]))
+            xg_codes.append(picked)
+        xg_scales = keep.tile([P, S], U8, name="xg_scales", align_bytes=64)
+        nc.vector.tensor_copy(xg_scales[:], x_scales[:].indirect(offs_t[:]))
+
+        z_codes, z_scales = [], []
+        w2_codes, w2_scales = [], []
+        for g in range(GROUPS):
+            acc = [psum.tile([P, S], F32, name=f"acc{g}_{t}", tag=f"bank{4 * g + t}") for t in range(4)]
+            for s in range(PASSES):
+                wb = keep.tile([P, 4, 128, 4], BF16, name=f"wb{g}_{s}", align_bytes=64)
+                w_codes = keep.tile([P, 512], U32, name=f"w_codes{g}_{s}", align_bytes=64)
+                w_scales = keep.tile([P, 512], U8, name=f"w_scales{g}_{s}", align_bytes=64)
+                last = g == GROUPS - 1 and s == PASSES - 1
+                step = 2 if last else 4
+                cut = W_SCALAR_LAST if last else W_SCALAR
+                for u in range(0, 4, step):
+                    dst = wb[:, u : u + step].rearrange("p t m j -> p m j t")
+                    src = w_raw[g][s][:].rearrange("p j (m t) -> p m j t", t=4)[:, :, :, u : u + step]
+                    nc.scalar.activation(dst[:, 0:cut], src[:, 0:cut], COPY)
+                    nc.vector.tensor_copy(dst[:, cut:128], src[:, cut:128])
+                    cols = slice(128 * u, 128 * (u + step))
+                    nc.vector.quantize_mx(
+                        out=w_codes[:, cols].bitcast(FP8X4),
+                        scales=w_scales[:, cols],
+                        in_=wb[:, u : u + step].rearrange("p t m j -> p (t m j)"),
+                    )
+                for t in range(4):
+                    cols = slice(128 * t, 128 * (t + 1))
+                    nc.tensor.matmul_mx(
+                        out=acc[t][:],
+                        lhsT=w_codes[:, cols].bitcast(FP8X4),
+                        lhsT_scale=w_scales[:, cols],
+                        rhs=xg_codes[s][:].bitcast(FP8X4),
+                        rhs_scale=xg_scales[4 * s : P, :],
+                        start=(s == 0),
+                        stop=(s == PASSES - 1),
+                    )
+            if g == GROUPS - 1:
+                for q in range(GROUPS):
+                    w2b = keep.tile([P, N, 4], BF16, name=f"w2b{q}", align_bytes=64)
+                    nc.vector.tensor_copy(
+                        w2b[:].rearrange("p (c i) j -> p c j i", i=4),
+                        w2_raw[:, q].rearrange("p j (c i) -> p c j i", i=4),
+                    )
+                    c2 = keep.tile([P, N], U32, name=f"w2_codes{q}", align_bytes=64)
+                    s2 = keep.tile([P, N], U8, name=f"w2_scales{q}", align_bytes=64)
+                    nc.vector.quantize_mx(
+                        out=c2[:].bitcast(FP8X4), scales=s2[:], in_=w2b[:].rearrange("p n j -> p (n j)")
+                    )
+                    w2_codes.append(c2)
+                    w2_scales.append(s2)
+            zc = keep.tile([P, V], U32, name=f"z_codes{g}", align_bytes=64)
+            zs = keep.tile([P, V], U8, name=f"z_scales{g}", align_bytes=64)
+            h = keep.tile([P, 4, V, 2], F32, name=f"h{g}")
+            zb = keep.tile([P, V, 4], BF16, name=f"zb{g}", align_bytes=64)
+            for half in range(2):
+                tok = slice(V * half, V * (half + 1))
+                pool = slice(V // 2 * half, V // 2 * (half + 1))
+                for t in range(4):
+                    nc.scalar.activation(
+                        h[:, t, pool, :].rearrange("p v d -> p (v d)"), acc[t][:, tok], SILU
+                    )
+                pairs = h[:, :, pool, :].rearrange("p t (c i) d -> p c t i d", i=2)
+                nc.vector.tensor_tensor(
+                    zb[:, pool, :].rearrange("p (c i) t -> p c t i", i=2),
+                    pairs[:, :, :, :, 0],
+                    pairs[:, :, :, :, 1],
+                    MAX,
+                )
+                nc.vector.quantize_mx(
+                    out=zc[:, pool].bitcast(FP8X4),
+                    scales=zs[:, pool],
+                    in_=zb[:, pool, :].rearrange("p v t -> p (v t)"),
+                )
+            z_codes.append(zc)
+            z_scales.append(zs)
+
+        for half in range(2):
+            pool = slice(V // 2 * half, V // 2 * (half + 1))
+            for a in range(N // P):
+                rows = slice(P * a, P * (a + 1))
+                acc2 = psum.tile([P, V // 2], F32, name=f"acc2_{half}_{a}", tag=f"bank{2 * half + a}")
+                for q in range(GROUPS):
+                    nc.tensor.matmul_mx(
+                        out=acc2[:],
+                        lhsT=w2_codes[q][:, rows].bitcast(FP8X4),
+                        lhsT_scale=w2_scales[q][:, rows],
+                        rhs=z_codes[q][:, pool].bitcast(FP8X4),
+                        rhs_scale=z_scales[q][:, pool],
+                        start=(q == 0),
+                        stop=(q == GROUPS - 1),
+                    )
+                gated = keep.tile([P, V // 2], F32, name=f"gated{half}_{a}")
+                nc.vector.tensor_tensor(gated[:], acc2[:], gate_t[:, a, pool], MULT)
+                nc.vector.tensor_copy(placed[a][:].indirect(pos_t[:, 8 * half : 8 * (half + 1)]), gated[:])
+        for a in range(N // P):
+            nc.sync.dma_start(out=out[P * a : P * (a + 1), :], in_=placed[a][:])

@@ -19,11 +19,10 @@ MAX = mybir.AluOpType.max
 P = 128
 PASSES = K // 512
 GROUPS = H // 512
-X_LOADS = ((0, 256), (256, 256), (512, 512))
-X_LOADS_LATER = ((0, 512), (512, 512))
-X_SCALAR = 5 / 8
-W_SCALAR = 80
-W_SCALAR_LAST = 56
+X_LOADS = (((0, 512), (512, 512)), ((0, 1024),), ((0, 1024),))
+X_STEP = 512
+X_SCALAR = (320, 384, 352)
+W_SCALAR = ((72, 64, 64), (64, 48, 56))
 
 
 def tile_picked_vpool_silu_e_kernel(tc, xT, w1, w2, gate, offs, pos1, out):
@@ -34,10 +33,9 @@ def tile_picked_vpool_silu_e_kernel(tc, xT, w1, w2, gate, offs, pos1, out):
 
         offs_t = keep.tile([P, S // 16], U16, name="offs_t")
         pos_t = keep.tile([P, V // 16], U16, name="pos_t")
-        x_loads = [X_LOADS if s == 0 else X_LOADS_LATER for s in range(PASSES)]
-        x_raw = [[keep.tile([P, 4, n], F32, name=f"x_raw{s}_{t0}") for t0, n in x_loads[s]] for s in range(PASSES)]
+        x_raw = [[keep.tile([P, 4, n], F32, name=f"x_raw{s}_{t0}") for t0, n in X_LOADS[s]] for s in range(PASSES)]
         w_raw = [[keep.tile([P, 4, 512], F32, name=f"w_raw{g}_{s}") for s in range(PASSES)] for g in range(GROUPS)]
-        w2_raw = keep.tile([P, GROUPS, 4, N], F32, name="w2_raw")
+        w2_raw = [keep.tile([P, 4, N], F32, name=f"w2_raw{q}") for q in range(GROUPS)]
         gate_t = keep.tile([P, N // P, V], F32, name="gate_t")
 
         warm = keep.tile([P, 1], F32, name="warm")
@@ -52,7 +50,7 @@ def tile_picked_vpool_silu_e_kernel(tc, xT, w1, w2, gate, offs, pos1, out):
             nc.gpsimd.memset(placed[a][:], 0.0)
 
         for s in range(PASSES):
-            for a, (t0, n) in enumerate(x_loads[s]):
+            for a, (t0, n) in enumerate(X_LOADS[s]):
                 nc.sync.dma_start(
                     out=x_raw[s][a][:],
                     in_=xT[512 * s : 512 * (s + 1), t0 : t0 + n].rearrange("(p j) t -> p j t", j=4),
@@ -65,26 +63,30 @@ def tile_picked_vpool_silu_e_kernel(tc, xT, w1, w2, gate, offs, pos1, out):
                     out=w_raw[g][s][:],
                     in_=w1[512 * s : 512 * (s + 1), 512 * g : 512 * (g + 1)].rearrange("(p j) c -> p j c", j=4),
                 )
-        nc.sync.dma_start(out=w2_raw[:], in_=w2.rearrange("(g p j) n -> p g j n", g=GROUPS, j=4))
+        for q in range(GROUPS):
+            nc.sync.dma_start(
+                out=w2_raw[q][:], in_=w2[512 * q : 512 * (q + 1), :].rearrange("(p j) n -> p j n", j=4)
+            )
         nc.sync.dma_start(pos_t[:], pos1)
         nc.sync.dma_start(out=gate_t[:], in_=gate.rearrange("(a p) v -> p a v", p=P))
 
         xg_codes = []
         for s in range(PASSES):
             x_codes = keep.tile([P, T], U32, name=f"x_codes{s}", align_bytes=64)
-            for a, (t0, n) in enumerate(x_loads[s]):
-                xb = keep.tile([P, n, 4], BF16, name=f"xb{s}_{a}", align_bytes=64)
-                dst = xb[:].rearrange("p (c i) j -> p c j i", i=4)
-                src = x_raw[s][a][:].rearrange("p j (c i) -> p c j i", i=4)
-                cut = int(n * X_SCALAR) // 4
-                nc.scalar.activation(dst[:, 0:cut], src[:, 0:cut], COPY)
-                nc.vector.tensor_copy(dst[:, cut : n // 4], src[:, cut : n // 4])
-                cols = slice(t0, t0 + n)
-                nc.vector.quantize_mx(
-                    out=x_codes[:, cols].bitcast(FP8X4),
-                    scales=x_scales[4 * s : P, cols],
-                    in_=xb[:].rearrange("p t j -> p (t j)"),
-                )
+            for (t0, n), raw in zip(X_LOADS[s], x_raw[s]):
+                for t1 in range(0, n, X_STEP):
+                    xb = keep.tile([P, X_STEP, 4], BF16, name=f"xb{s}_{t0 + t1}", align_bytes=64)
+                    dst = xb[:].rearrange("p (c i) j -> p c j i", i=4)
+                    src = raw[:, :, t1 : t1 + X_STEP].rearrange("p j (c i) -> p c j i", i=4)
+                    cut = X_SCALAR[s] // 4
+                    nc.scalar.activation(dst[:, 0:cut], src[:, 0:cut], COPY)
+                    nc.vector.tensor_copy(dst[:, cut:], src[:, cut:])
+                    cols = slice(t0 + t1, t0 + t1 + X_STEP)
+                    nc.vector.quantize_mx(
+                        out=x_codes[:, cols].bitcast(FP8X4),
+                        scales=x_scales[4 * s : P, cols],
+                        in_=xb[:].rearrange("p t j -> p (t j)"),
+                    )
             picked = keep.tile([P, S], U32, name=f"xg_codes{s}", align_bytes=64)
             nc.vector.tensor_copy(picked[:], x_codes[:].indirect(offs_t[:]))
             xg_codes.append(picked)
@@ -101,7 +103,7 @@ def tile_picked_vpool_silu_e_kernel(tc, xT, w1, w2, gate, offs, pos1, out):
                 w_scales = keep.tile([P, 512], U8, name=f"w_scales{g}_{s}", align_bytes=64)
                 last = g == GROUPS - 1 and s == PASSES - 1
                 step = 2 if last else 4
-                cut = W_SCALAR_LAST if last else W_SCALAR
+                cut = W_SCALAR[g][s]
                 for u in range(0, 4, step):
                     dst = wb[:, u : u + step].rearrange("p t m j -> p m j t")
                     src = w_raw[g][s][:].rearrange("p j (m t) -> p m j t", t=4)[:, :, :, u : u + step]
@@ -129,7 +131,7 @@ def tile_picked_vpool_silu_e_kernel(tc, xT, w1, w2, gate, offs, pos1, out):
                     w2b = keep.tile([P, N, 4], BF16, name=f"w2b{q}", align_bytes=64)
                     nc.vector.tensor_copy(
                         w2b[:].rearrange("p (c i) j -> p c j i", i=4),
-                        w2_raw[:, q].rearrange("p j (c i) -> p c j i", i=4),
+                        w2_raw[q][:].rearrange("p j (c i) -> p c j i", i=4),
                     )
                     c2 = keep.tile([P, N], U32, name=f"w2_codes{q}", align_bytes=64)
                     s2 = keep.tile([P, N], U8, name=f"w2_scales{q}", align_bytes=64)
@@ -179,8 +181,10 @@ def tile_picked_vpool_silu_e_kernel(tc, xT, w1, w2, gate, offs, pos1, out):
                         start=(q == 0),
                         stop=(q == GROUPS - 1),
                     )
-                gated = keep.tile([P, V // 2], F32, name=f"gated{half}_{a}")
-                nc.vector.tensor_tensor(gated[:], acc2[:], gate_t[:, a, pool], MULT)
-                nc.vector.tensor_copy(placed[a][:].indirect(pos_t[:, 8 * half : 8 * (half + 1)]), gated[:])
+                result = keep.tile([P, V // 2], F32, name=f"result{half}_{a}")
+                nc.scalar.activation(result[:], acc2[:], COPY)
+                nc.vector.tensor_tensor(
+                    placed[a][:].indirect(pos_t[:, 8 * half : 8 * (half + 1)]), result[:], gate_t[:, a, pool], MULT
+                )
         for a in range(N // P):
             nc.sync.dma_start(out=out[P * a : P * (a + 1), :], in_=placed[a][:])

@@ -19,10 +19,10 @@ MAX = mybir.AluOpType.max
 P = 128
 PASSES = K // 512
 GROUPS = H // 512
-X_LOADS = (((0, 512), (512, 512)), ((0, 1024),), ((0, 1024),))
 X_STEP = 512
-X_SCALAR = (320, 384, 352)
-W_SCALAR = ((72, 64, 64), (64, 48, 56))
+X_SCALAR = 256
+W_LOADS = ((0, 0, 2), (1, 0, 1), (2, 0, 1), (1, 1, 1), (2, 1, 1))
+W_SCALAR = ((64, 64, 64), (64, 64, 48))
 
 
 def tile_picked_vpool_silu_e_kernel(tc, xT, w1, w2, gate, offs, pos1, out):
@@ -33,8 +33,8 @@ def tile_picked_vpool_silu_e_kernel(tc, xT, w1, w2, gate, offs, pos1, out):
 
         offs_t = keep.tile([P, S // 16], U16, name="offs_t")
         pos_t = keep.tile([P, V // 16], U16, name="pos_t")
-        x_raw = [[keep.tile([P, 4, n], F32, name=f"x_raw{s}_{t0}") for t0, n in X_LOADS[s]] for s in range(PASSES)]
-        w_raw = [[keep.tile([P, 4, 512], F32, name=f"w_raw{g}_{s}") for s in range(PASSES)] for g in range(GROUPS)]
+        x_raw = [keep.tile([P, 4, T], F32, name=f"x_raw{s}") for s in range(PASSES)]
+        w_raw = [keep.tile([P, 4, 512 * gs], F32, name=f"w_raw{g0}_{s}") for s, g0, gs in W_LOADS]
         w2_raw = [keep.tile([P, 4, N], F32, name=f"w2_raw{q}") for q in range(GROUPS)]
         gate_t = keep.tile([P, N // P, V], F32, name="gate_t")
 
@@ -50,19 +50,16 @@ def tile_picked_vpool_silu_e_kernel(tc, xT, w1, w2, gate, offs, pos1, out):
             nc.gpsimd.memset(placed[a][:], 0.0)
 
         for s in range(PASSES):
-            for a, (t0, n) in enumerate(X_LOADS[s]):
-                nc.sync.dma_start(
-                    out=x_raw[s][a][:],
-                    in_=xT[512 * s : 512 * (s + 1), t0 : t0 + n].rearrange("(p j) t -> p j t", j=4),
-                )
-                if s == 0 and a == 1:
-                    nc.sync.dma_start(offs_t[:], offs)
-        for g in range(GROUPS):
-            for s in range(PASSES):
-                nc.sync.dma_start(
-                    out=w_raw[g][s][:],
-                    in_=w1[512 * s : 512 * (s + 1), 512 * g : 512 * (g + 1)].rearrange("(p j) c -> p j c", j=4),
-                )
+            nc.sync.dma_start(
+                out=x_raw[s][:], in_=xT[512 * s : 512 * (s + 1), :].rearrange("(p j) t -> p j t", j=4)
+            )
+            if s == 0:
+                nc.sync.dma_start(offs_t[:], offs)
+        for raw, (s, g0, gs) in zip(w_raw, W_LOADS):
+            nc.sync.dma_start(
+                out=raw[:],
+                in_=w1[512 * s : 512 * (s + 1), 512 * g0 : 512 * (g0 + gs)].rearrange("(p j) c -> p j c", j=4),
+            )
         for q in range(GROUPS):
             nc.sync.dma_start(
                 out=w2_raw[q][:], in_=w2[512 * q : 512 * (q + 1), :].rearrange("(p j) n -> p j n", j=4)
@@ -73,20 +70,19 @@ def tile_picked_vpool_silu_e_kernel(tc, xT, w1, w2, gate, offs, pos1, out):
         xg_codes = []
         for s in range(PASSES):
             x_codes = keep.tile([P, T], U32, name=f"x_codes{s}", align_bytes=64)
-            for (t0, n), raw in zip(X_LOADS[s], x_raw[s]):
-                for t1 in range(0, n, X_STEP):
-                    xb = keep.tile([P, X_STEP, 4], BF16, name=f"xb{s}_{t0 + t1}", align_bytes=64)
-                    dst = xb[:].rearrange("p (c i) j -> p c j i", i=4)
-                    src = raw[:, :, t1 : t1 + X_STEP].rearrange("p j (c i) -> p c j i", i=4)
-                    cut = X_SCALAR[s] // 4
-                    nc.scalar.activation(dst[:, 0:cut], src[:, 0:cut], COPY)
-                    nc.vector.tensor_copy(dst[:, cut:], src[:, cut:])
-                    cols = slice(t0 + t1, t0 + t1 + X_STEP)
-                    nc.vector.quantize_mx(
-                        out=x_codes[:, cols].bitcast(FP8X4),
-                        scales=x_scales[4 * s : P, cols],
-                        in_=xb[:].rearrange("p t j -> p (t j)"),
-                    )
+            for t0 in range(0, T, X_STEP):
+                xb = keep.tile([P, X_STEP, 4], BF16, name=f"xb{s}_{t0}", tag=f"xb{t0}", align_bytes=64)
+                cols = slice(t0, t0 + X_STEP)
+                dst = xb[:].rearrange("p (c i) j -> p c j i", i=4)
+                src = x_raw[s][:, :, cols].rearrange("p j (c i) -> p c j i", i=4)
+                cut = X_SCALAR // 4
+                nc.scalar.activation(dst[:, 0:cut], src[:, 0:cut], COPY)
+                nc.vector.tensor_copy(dst[:, cut:], src[:, cut:])
+                nc.vector.quantize_mx(
+                    out=x_codes[:, cols].bitcast(FP8X4),
+                    scales=x_scales[4 * s : P, cols],
+                    in_=xb[:].rearrange("p t j -> p (t j)"),
+                )
             picked = keep.tile([P, S], U32, name=f"xg_codes{s}", align_bytes=64)
             nc.vector.tensor_copy(picked[:], x_codes[:].indirect(offs_t[:]))
             xg_codes.append(picked)
@@ -95,37 +91,42 @@ def tile_picked_vpool_silu_e_kernel(tc, xT, w1, w2, gate, offs, pos1, out):
 
         z_codes, z_scales = [], []
         w2_codes, w2_scales = [], []
+        accs = [
+            [psum.tile([P, S], F32, name=f"acc{g}_{t}", tag=f"bank{4 * g + t}") for t in range(4)]
+            for g in range(GROUPS)
+        ]
+        pieces = [(raw, s, g, g - g0) for raw, (s, g0, gs) in zip(w_raw, W_LOADS) for g in range(g0, g0 + gs)]
+        for n, (raw, s, g, part) in enumerate(pieces):
+            wb = keep.tile([P, 4, 128, 4], BF16, name=f"wb{g}_{s}", align_bytes=64)
+            w_codes = keep.tile([P, 512], U32, name=f"w_codes{g}_{s}", align_bytes=64)
+            w_scales = keep.tile([P, 512], U8, name=f"w_scales{g}_{s}", align_bytes=64)
+            step = 2 if n == len(pieces) - 1 else 4
+            cut = W_SCALAR[g][s]
+            for u in range(0, 4, step):
+                dst = wb[:, u : u + step].rearrange("p t m j -> p m j t")
+                src = raw[:, :, 512 * part : 512 * (part + 1)].rearrange("p j (m t) -> p m j t", t=4)
+                src = src[:, :, :, u : u + step]
+                nc.scalar.activation(dst[:, 0:cut], src[:, 0:cut], COPY)
+                nc.vector.tensor_copy(dst[:, cut:128], src[:, cut:128])
+                cols = slice(128 * u, 128 * (u + step))
+                nc.vector.quantize_mx(
+                    out=w_codes[:, cols].bitcast(FP8X4),
+                    scales=w_scales[:, cols],
+                    in_=wb[:, u : u + step].rearrange("p t m j -> p (t m j)"),
+                )
+            for t in range(4):
+                cols = slice(128 * t, 128 * (t + 1))
+                nc.tensor.matmul_mx(
+                    out=accs[g][t][:],
+                    lhsT=w_codes[:, cols].bitcast(FP8X4),
+                    lhsT_scale=w_scales[:, cols],
+                    rhs=xg_codes[s][:].bitcast(FP8X4),
+                    rhs_scale=xg_scales[4 * s : P, :],
+                    start=(s == 0),
+                    stop=(s == PASSES - 1),
+                )
         for g in range(GROUPS):
-            acc = [psum.tile([P, S], F32, name=f"acc{g}_{t}", tag=f"bank{4 * g + t}") for t in range(4)]
-            for s in range(PASSES):
-                wb = keep.tile([P, 4, 128, 4], BF16, name=f"wb{g}_{s}", align_bytes=64)
-                w_codes = keep.tile([P, 512], U32, name=f"w_codes{g}_{s}", align_bytes=64)
-                w_scales = keep.tile([P, 512], U8, name=f"w_scales{g}_{s}", align_bytes=64)
-                last = g == GROUPS - 1 and s == PASSES - 1
-                step = 2 if last else 4
-                cut = W_SCALAR[g][s]
-                for u in range(0, 4, step):
-                    dst = wb[:, u : u + step].rearrange("p t m j -> p m j t")
-                    src = w_raw[g][s][:].rearrange("p j (m t) -> p m j t", t=4)[:, :, :, u : u + step]
-                    nc.scalar.activation(dst[:, 0:cut], src[:, 0:cut], COPY)
-                    nc.vector.tensor_copy(dst[:, cut:128], src[:, cut:128])
-                    cols = slice(128 * u, 128 * (u + step))
-                    nc.vector.quantize_mx(
-                        out=w_codes[:, cols].bitcast(FP8X4),
-                        scales=w_scales[:, cols],
-                        in_=wb[:, u : u + step].rearrange("p t m j -> p (t m j)"),
-                    )
-                for t in range(4):
-                    cols = slice(128 * t, 128 * (t + 1))
-                    nc.tensor.matmul_mx(
-                        out=acc[t][:],
-                        lhsT=w_codes[:, cols].bitcast(FP8X4),
-                        lhsT_scale=w_scales[:, cols],
-                        rhs=xg_codes[s][:].bitcast(FP8X4),
-                        rhs_scale=xg_scales[4 * s : P, :],
-                        start=(s == 0),
-                        stop=(s == PASSES - 1),
-                    )
+            acc = accs[g]
             if g == GROUPS - 1:
                 for q in range(GROUPS):
                     w2b = keep.tile([P, N, 4], BF16, name=f"w2b{q}", align_bytes=64)

@@ -22,7 +22,7 @@ GROUPS = H // 512
 X_STEP = 512
 X_SCALAR = 256
 W_LOADS = ((0, 0, 2), (1, 0, 1), (2, 0, 1), (1, 1, 1), (2, 1, 1))
-W_SCALAR = ((64, 64, 64), (64, 64, 48))
+W_SCALAR = ((72, 72, 72), (72, 56, 48))
 
 
 def tile_picked_vpool_silu_e_kernel(tc, xT, w1, w2, gate, offs, pos1, out):
@@ -169,6 +169,7 @@ def tile_picked_vpool_silu_e_kernel(tc, xT, w1, w2, gate, offs, pos1, out):
 
         for half in range(2):
             pool = slice(V // 2 * half, V // 2 * (half + 1))
+            gated = []
             for a in range(N // P):
                 rows = slice(P * a, P * (a + 1))
                 acc2 = psum.tile([P, V // 2], F32, name=f"acc2_{half}_{a}", tag=f"bank{2 * half + a}")
@@ -182,10 +183,10 @@ def tile_picked_vpool_silu_e_kernel(tc, xT, w1, w2, gate, offs, pos1, out):
                         start=(q == 0),
                         stop=(q == GROUPS - 1),
                     )
-                result = keep.tile([P, V // 2], F32, name=f"result{half}_{a}")
-                nc.scalar.activation(result[:], acc2[:], COPY)
-                nc.vector.tensor_tensor(
-                    placed[a][:].indirect(pos_t[:, 8 * half : 8 * (half + 1)]), result[:], gate_t[:, a, pool], MULT
-                )
+                weighted = keep.tile([P, V // 2], F32, name=f"weighted{half}_{a}")
+                nc.vector.tensor_tensor(weighted[:], acc2[:], gate_t[:, a, pool], MULT)
+                gated.append(weighted)
+            for a in range(N // P):
+                nc.vector.tensor_copy(placed[a][:].indirect(pos_t[:, 8 * half : 8 * (half + 1)]), gated[a][:])
         for a in range(N // P):
             nc.sync.dma_start(out=out[P * a : P * (a + 1), :], in_=placed[a][:])

from contextlib import ExitStack

import concourse.mybir as mybir

K, T, D, S, V, H, N = 1536, 1024, 2, 512, 256, 1024, 256
FLOPS = 2 * K * S * H + 2 * H * V * N

F32 = mybir.dt.float32
BF16 = mybir.dt.bfloat16
U32 = mybir.dt.uint32
U16 = mybir.dt.uint16
U8 = mybir.dt.uint8
FP8X4 = mybir.dt.float8_e4m3fn_x4
SILU = mybir.ActivationFunctionType.Silu
COPY = mybir.ActivationFunctionType.Copy
MULT = mybir.AluOpType.mult
MAX = mybir.AluOpType.max

P = 128
PASSES = K // 512
GROUPS = H // 512
X_STEP = 512
X_SCALAR = 256
W_LOADS = ((0, 0, 2), (1, 0, 1), (2, 0, 1), (1, 1, 1), (2, 1, 1))
W_SCALAR = ((72, 72, 72), (72, 56, 48))


def tile_picked_vpool_silu_e_kernel(tc, xT, w1, w2, gate, offs, pos1, out):
    nc = tc.nc
    with ExitStack() as ctx:
        keep = ctx.enter_context(tc.tile_pool(name="keep", bufs=1))
        psum = ctx.enter_context(tc.psum_pool(name="psum", bufs=1))

        offs_t = keep.tile([P, S // 16], U16, name="offs_t")
        pos_t = keep.tile([P, V // 16], U16, name="pos_t")
        x_raw = [keep.tile([P, 4, T], F32, name=f"x_raw{s}") for s in range(PASSES)]
        w_raw = [keep.tile([P, 4, 512 * gs], F32, name=f"w_raw{g0}_{s}") for s, g0, gs in W_LOADS]
        w2_raw = [keep.tile([P, 4, N], F32, name=f"w2_raw{q}") for q in range(GROUPS)]
        gate_t = keep.tile([P, N // P, V], F32, name="gate_t")

        warm = keep.tile([P, 1], F32, name="warm")
        warm_out = keep.tile([P, 1], F32, name="warm_out")
        nc.gpsimd.memset(warm[:], 0.0)
        nc.scalar.activation(warm_out[:], warm[:], SILU)

        x_scales = keep.tile([P, T], U8, name="x_scales", align_bytes=64)
        nc.gpsimd.memset(x_scales[:], 0)
        placed = [keep.tile([P, 2 * V], F32, name=f"placed{a}") for a in range(N // P)]
        for a in range(N // P):
            nc.gpsimd.memset(placed[a][:], 0.0)

        for s in range(PASSES):
            nc.sync.dma_start(
                out=x_raw[s][:], in_=xT[512 * s : 512 * (s + 1), :].rearrange("(p j) t -> p j t", j=4)
            )
            if s == 0:
                nc.sync.dma_start(offs_t[:], offs)
        for raw, (s, g0, gs) in zip(w_raw, W_LOADS):
            nc.sync.dma_start(
                out=raw[:],
                in_=w1[512 * s : 512 * (s + 1), 512 * g0 : 512 * (g0 + gs)].rearrange("(p j) c -> p j c", j=4),
            )
        for q in range(GROUPS):
            nc.sync.dma_start(
                out=w2_raw[q][:], in_=w2[512 * q : 512 * (q + 1), :].rearrange("(p j) n -> p j n", j=4)
            )
        nc.sync.dma_start(pos_t[:], pos1)
        nc.sync.dma_start(out=gate_t[:], in_=gate.rearrange("(a p) v -> p a v", p=P))

        xg_codes = []
        for s in range(PASSES):
            x_codes = keep.tile([P, T], U32, name=f"x_codes{s}", align_bytes=64)
            for t0 in range(0, T, X_STEP):
                xb = keep.tile([P, X_STEP, 4], BF16, name=f"xb{s}_{t0}", tag=f"xb{t0}", align_bytes=64)
                cols = slice(t0, t0 + X_STEP)
                dst = xb[:].rearrange("p (c i) j -> p c j i", i=4)
                src = x_raw[s][:, :, cols].rearrange("p j (c i) -> p c j i", i=4)
                cut = X_SCALAR // 4
                nc.scalar.activation(dst[:, 0:cut], src[:, 0:cut], COPY)
                nc.vector.tensor_copy(dst[:, cut:], src[:, cut:])
                nc.vector.quantize_mx(
                    out=x_codes[:, cols].bitcast(FP8X4),
                    scales=x_scales[4 * s : P, cols],
                    in_=xb[:].rearrange("p t j -> p (t j)"),
                )
            picked = keep.tile([P, S], U32, name=f"xg_codes{s}", align_bytes=64)
            nc.vector.tensor_copy(picked[:], x_codes[:].indirect(offs_t[:]))
            xg_codes.append(picked)
        xg_scales = keep.tile([P, S], U8, name="xg_scales", align_bytes=64)
        nc.vector.tensor_copy(xg_scales[:], x_scales[:].indirect(offs_t[:]))

        z_codes, z_scales = [], []
        w2_codes, w2_scales = [], []
        accs = [
            [psum.tile([P, S], F32, name=f"acc{g}_{t}", tag=f"bank{4 * g + t}") for t in range(4)]
            for g in range(GROUPS)
        ]
        pieces = [(raw, s, g, g - g0) for raw, (s, g0, gs) in zip(w_raw, W_LOADS) for g in range(g0, g0 + gs)]
        for n, (raw, s, g, part) in enumerate(pieces):
            wb = keep.tile([P, 4, 128, 4], BF16, name=f"wb{g}_{s}", align_bytes=64)
            w_codes = keep.tile([P, 512], U32, name=f"w_codes{g}_{s}", align_bytes=64)
            w_scales = keep.tile([P, 512], U8, name=f"w_scales{g}_{s}", align_bytes=64)
            step = 2 if n == len(pieces) - 1 else 4
            cut = W_SCALAR[g][s]
            for u in range(0, 4, step):
                dst = wb[:, u : u + step].rearrange("p t m j -> p m j t")
                src = raw[:, :, 512 * part : 512 * (part + 1)].rearrange("p j (m t) -> p m j t", t=4)
                src = src[:, :, :, u : u + step]
                nc.scalar.activation(dst[:, 0:cut], src[:, 0:cut], COPY)
                nc.vector.tensor_copy(dst[:, cut:128], src[:, cut:128])
                cols = slice(128 * u, 128 * (u + step))
                nc.vector.quantize_mx(
                    out=w_codes[:, cols].bitcast(FP8X4),
                    scales=w_scales[:, cols],
                    in_=wb[:, u : u + step].rearrange("p t m j -> p (t m j)"),
                )
            for t in range(4):
                cols = slice(128 * t, 128 * (t + 1))
                nc.tensor.matmul_mx(
                    out=accs[g][t][:],
                    lhsT=w_codes[:, cols].bitcast(FP8X4),
                    lhsT_scale=w_scales[:, cols],
                    rhs=xg_codes[s][:].bitcast(FP8X4),
                    rhs_scale=xg_scales[4 * s : P, :],
                    start=(s == 0),
                    stop=(s == PASSES - 1),
                )
        for g in range(GROUPS):
            acc = accs[g]
            if g == GROUPS - 1:
                for q in range(GROUPS):
                    w2b = keep.tile([P, N, 4], BF16, name=f"w2b{q}", align_bytes=64)
                    nc.vector.tensor_copy(
                        w2b[:].rearrange("p (c i) j -> p c j i", i=4),
                        w2_raw[q][:].rearrange("p j (c i) -> p c j i", i=4),
                    )
                    c2 = keep.tile([P, N], U32, name=f"w2_codes{q}", align_bytes=64)
                    s2 = keep.tile([P, N], U8, name=f"w2_scales{q}", align_bytes=64)
                    nc.vector.quantize_mx(
                        out=c2[:].bitcast(FP8X4), scales=s2[:], in_=w2b[:].rearrange("p n j -> p (n j)")
                    )
                    w2_codes.append(c2)
                    w2_scales.append(s2)
            zc = keep.tile([P, V], U32, name=f"z_codes{g}", align_bytes=64)
            zs = keep.tile([P, V], U8, name=f"z_scales{g}", align_bytes=64)
            h = keep.tile([P, 4, V, 2], F32, name=f"h{g}")
            zb = keep.tile([P, V, 4], BF16, name=f"zb{g}", align_bytes=64)
            for half in range(2):
                tok = slice(V * half, V * (half + 1))
                pool = slice(V // 2 * half, V // 2 * (half + 1))
                for t in range(4):
                    nc.scalar.activation(
                        h[:, t, pool, :].rearrange("p v d -> p (v d)"), acc[t][:, tok], SILU
                    )
                pairs = h[:, :, pool, :].rearrange("p t (c i) d -> p c t i d", i=2)
                nc.vector.tensor_tensor(
                    zb[:, pool, :].rearrange("p (c i) t -> p c t i", i=2),
                    pairs[:, :, :, :, 0],
                    pairs[:, :, :, :, 1],
                    MAX,
                )
                nc.vector.quantize_mx(
                    out=zc[:, pool].bitcast(FP8X4),
                    scales=zs[:, pool],
                    in_=zb[:, pool, :].rearrange("p v t -> p (v t)"),
                )
            z_codes.append(zc)
            z_scales.append(zs)

        for half in range(2):
            pool = slice(V // 2 * half, V // 2 * (half + 1))
            gated = []
            for a in range(N // P):
                rows = slice(P * a, P * (a + 1))
                acc2 = psum.tile([P, V // 2], F32, name=f"acc2_{half}_{a}", tag=f"bank{2 * half + a}")
                for q in range(GROUPS):
                    nc.tensor.matmul_mx(
                        out=acc2[:],
                        lhsT=w2_codes[q][:, rows].bitcast(FP8X4),
                        lhsT_scale=w2_scales[q][:, rows],
                        rhs=z_codes[q][:, pool].bitcast(FP8X4),
                        rhs_scale=z_scales[q][:, pool],
                        start=(q == 0),
                        stop=(q == GROUPS - 1),
                    )
                weighted = keep.tile([P, V // 2], F32, name=f"weighted{half}_{a}")
                nc.vector.tensor_tensor(weighted[:], acc2[:], gate_t[:, a, pool], MULT)
                gated.append(weighted)
            for a in range(N // P):
                nc.vector.tensor_copy(placed[a][:].indirect(pos_t[:, 8 * half : 8 * (half + 1)]), gated[a][:])
        for a in range(N // P):
            nc.sync.dma_start(out=out[P * a : P * (a + 1), :], in_=placed[a][:])
